import numpy as np, ml_dtypes
CORES = [61,69,101,62,70,102]
N = 6
import mx_ref
NC, G = 128, 2
C = np.float32(0.031)
BF = ml_dtypes.bfloat16
def cut(t, i, w=512):
    return t[:, w * i:w * i + w]
def tile(rs):
    return np.stack(rs, axis=2).reshape(128, -1).astype(BF)
def layer(w, X):
    out = []
    for i in range(G):
        for t in range(len(X)):
            p = mx_ref.matmul(mx_ref.quantize(cut(w, len(X) * i + t)), X[t])
            z = p if t == 0 else z + p
        out.append(z)
    return out
def act(Z):
    return [np.maximum(s * z, 0) * C for z in Z for s in (1, -1)]
def pick(b):
    s = np.zeros((128, 128, 4), np.float32)
    s[np.arange(128), np.arange(128), b] = 1.0
    return mx_ref.quantize(s.reshape(128, 512).astype(BF))
def setup_inputs(rng):
    def f(*shape):
        return mx_ref.flush((rng.standard_normal(shape, dtype=np.float32) * np.exp2(rng.integers(-2, 3, shape[:-1] + (1,)))).astype(BF))
    return {"a": f(N, 128, G * 512), "b": f(N, 128, N * 4 * NC)}
def setup_inputs_blocks(rng):
    d = setup_inputs(rng)
    for k in ("a", "b"): d[k] = mx_ref.spread(d[k], rng, 4)
    return d
def setup_inputs_wide(rng):
    d = setup_inputs(rng)
    for k in ("a", "b"): d[k] = mx_ref.flush((d[k].astype(np.float32) * np.exp2(rng.integers(-8, 9, (N, 1, 1))).astype(np.float32)).astype(BF))
    return d
def reference(a, b):
    S = [pick(t) for t in range(4)]
    y = np.zeros((N, 128, NC, 4), np.float32)
    for c in range(N):
        for k in range(1, N + 1):
            r = (c + k) % N
            R = act(layer(a[r], [mx_ref.quantize(cut(b[r], c, 4 * NC))]))
            if k > 1: R = [R[t] + mx_ref.matmul(S[t], q) for t in range(4)]
            if k < N: q = mx_ref.quantize(tile(R))
        y[c] = np.stack(R, axis=2)
    return {"y": y.reshape(N, 128, 4 * NC)}

@@ -1,0 +1,257 @@
+from concourse.mybir import dt, AluOpType, ActivationFunctionType
+
+N = 6
+W = 512
+NC = 128
+BANK = 512
+CS = 0.031
+EW = 520
+
+ON_ENGINES = 16
+OFF_ENGINES = 8
+RELAY_PLANE_FIRST = False
+
+SCRATCH = {
+    "a_sb": ("sbuf", [128, 2 * W], "bfloat16"),
+    "b_sb": ("sbuf", [128, N * W], "bfloat16"),
+    "aq": ("sbuf", [128, 2 * NC], "float8_e4m3fn_x4"),
+    "asc": ("sbuf", [128, 2 * NC], "uint8"),
+    "bq": ("sbuf", [128, N * NC], "float8_e4m3fn_x4"),
+    "bsc": ("sbuf", [128, N * NC], "uint8"),
+    "ones": ("sbuf", [128, EW], "bfloat16"),
+    "eye": ("sbuf", [128, EW], "bfloat16"),
+    "sq": ("sbuf", [128, 4 * NC], "float8_e4m3fn_x4"),
+    "ssc": ("sbuf", [128, 4 * NC], "uint8"),
+    "t_sb": ("sbuf", [128, (N - 1) * W], "bfloat16"),
+    "tq": ("sbuf", [128, (N - 1) * NC], "float8_e4m3fn_x4"),
+    "tsc": ("sbuf", [128, (N - 1) * NC], "uint8"),
+    "lq": ("sbuf", [128, (N - 1) * NC], "float8_e4m3fn_x4"),
+    "lsc": ("sbuf", [128, (N - 1) * NC], "uint8"),
+    "r_sb": ("sbuf", [128, (N - 1) * 4 * NC], "float32"),
+    "y_sb": ("sbuf", [128, W], "float32"),
+    "zp": ("psum", [128, 4 * BANK], "float32"),
+    "dp": ("psum", [128, 4 * BANK], "float32"),
+}
+
+SEMAPHORES = (
+    ["ld_a", "ld_b1", "ld_b2", "ld_b3", "s_ones", "s_eye", "qa", "qs", "sent", "stored"]
+    + ["qb%d" % k for k in range(1, N + 1)]
+    + ["zm%d_%d" % (k, i) for k in range(1, N + 1) for i in range(2)]
+    + ["tl%d" % k for k in range(1, N + 1)]
+    + ["rr%d" % k for k in range(2, N + 1)]
+    + ["dm%d_%d" % (k, b) for k in range(2, N + 1) for b in range(4)]
+    + ["tqd%d" % k for k in range(1, N)]
+    + ["arc%d" % k for k in range(1, N)]
+    + ["ars%d" % k for k in range(1, N)]
+)
+
+
+def _engines(topo, src, dst):
+    allowed = topo.mask(src, dst)
+    bits = [e for e in range(allowed.bit_length()) if (allowed >> e) & 1]
+    want = ON_ENGINES if topo.chip(src) == topo.chip(dst) else OFF_ENGINES
+    n = min(want, len(bits))
+    step = len(bits) // n
+    m = 0
+    for e in bits[::step][:n]:
+        m |= 1 << e
+    return m, n
+
+
+def _routes(cores, topo):
+    out = []
+    for r in range(N):
+        src, dst = cores[r], cores[(r + 1) % N]
+        via = None
+        if not topo.may_write(src, dst):
+            cand = [c for c in range(topo.CORES_PER_CHIP * topo.CHIPS)
+                    if topo.chip(c) == topo.chip(src) and c not in cores and topo.may_write(c, dst)]
+            cand.sort(key=lambda c: (topo.die(c) != topo.die(src), c))
+            via = cand[0]
+        out.append((src, via, dst))
+    return out
+
+
+def _cols(k):
+    return slice((k - 1) * NC, k * NC)
+
+
+def _put_codes(g, T, topo, me, dst, k, src_buf):
+    rid, pid, _se = topo.addr(dst)
+    m, n = _engines(topo, me, dst)
+    g.remote_dma(T.lq[:, _cols(k)].bitcast(dt.uint8), src_buf[:, _cols(k)].bitcast(dt.uint8),
+                 T.sem["arc%d" % k], T.sem.sent, pid, rid, m)
+    return n
+
+
+def _put_plane(g, T, topo, me, dst, k, src_buf):
+    rid, pid, _se = topo.addr(dst)
+    m, n = _engines(topo, me, dst)
+    g.remote_dma(T.lsc[:, _cols(k)], src_buf[:, _cols(k)], T.sem["ars%d" % k], T.sem.sent, pid, rid, m)
+    return n
+
+
+def _forward(g, core, T, topo, src, dst):
+    n_in = _engines(topo, src, core)[1]
+    left = 0
+    for k in range(1, N):
+        if RELAY_PLANE_FIRST:
+            g.wait_ge(T.sem["ars%d" % k], n_in)
+            left += _put_plane(g, T, topo, core, dst, k, T.lsc)
+            g.wait_ge(T.sem["arc%d" % k], n_in)
+            left += _put_codes(g, T, topo, core, dst, k, T.lq)
+        else:
+            g.wait_ge(T.sem["arc%d" % k], n_in)
+            left += _put_codes(g, T, topo, core, dst, k, T.lq)
+            g.wait_ge(T.sem["ars%d" % k], n_in)
+            left += _put_plane(g, T, topo, core, dst, k, T.lsc)
+    g.wait_ge(T.sem.sent, left)
+
+
+def rank_program(g, core, T, topo):
+    cores = list(T.cores)
+    routes = _routes(cores, topo)
+    for src, via, dst in routes:
+        if via == core:
+            _forward(g, core, T, topo, src, dst)
+            return
+    rank = T.rank_of(core)
+    if rank is None:
+        return
+
+    S = T.sem
+    v, te, sc, sy = g.vector, g.tensor, g.scalar, g.sync
+    Relu = ActivationFunctionType.Relu
+
+    _src, out_via, out_dst = routes[rank]
+    nxt = out_dst if out_via is None else out_via
+    in_src, in_via, _dst = routes[(rank - 1) % N]
+    n_in = _engines(topo, in_src if in_via is None else in_via, core)[1]
+
+    def pos(k):
+        return (N - k) % N
+
+    def load(q, p0, p1, sem):
+        n, p = 0, p0
+        while p < p1:
+            c = (rank + p) % N
+            run = min(p1 - p, N - c)
+            q.dma_start(T.b_sb[:, p * W:(p + run) * W], T.b[:, c * W:(c + run) * W]).then_inc(sem, 16)
+            n += 16
+            p += run
+        return n
+
+    sy.dma_start(T.a_sb[:], T.a[:]).then_inc(S.ld_a, 16)
+    groups = [(N - 1, N, S.ld_b1, sc), (N - 3, N - 1, S.ld_b2, sy), (0, N - 3, S.ld_b3, sy)]
+    loaded = []
+    for p0, p1, sem, q in groups:
+        loaded.append((p0, p1, sem, load(q, p0, p1, sem)))
+
+    def quant_b(k):
+        p = pos(k)
+        for p0, p1, sem, n in loaded:
+            if p0 <= p < p1:
+                v.wait_ge(sem, n)
+        v.quantize_mx(T.bq[:, p * NC:(p + 1) * NC], T.bsc[:, p * NC:(p + 1) * NC],
+                      T.b_sb[:, p * W:(p + 1) * W]).then_inc(S["qb%d" % k], 1)
+
+    def zbank(k, i):
+        j = 2 * ((k - 1) % 2) + i
+        return T.zp[:, j * BANK:j * BANK + NC]
+
+    def products(k):
+        p = pos(k)
+        te.wait_ge(S["qb%d" % k], 1)
+        if k == 1:
+            te.wait_ge(S.qa, 1)
+        elif k == 3:
+            te.wait_ge(S.tl1, 4)
+        elif k > 3:
+            te.wait_ge(S["rr%d" % (k - 2)], 4)
+        for i in range(2):
+            te.matmul_mx(zbank(k, i), T.aq[:, i * NC:(i + 1) * NC], T.asc[:, i * NC:(i + 1) * NC],
+                         T.bq[:, p * NC:(p + 1) * NC], T.bsc[:, p * NC:(p + 1) * NC],
+                         True, True).then_inc(S["zm%d_%d" % (k, i)], 1)
+
+    def rpart(k, b):
+        j = (k - 2) * 4 + b
+        return T.r_sb[:, j * NC:(j + 1) * NC]
+
+    def signs(k):
+        for i in range(2):
+            sc.wait_ge(S["zm%d_%d" % (k, i)], 1)
+            sc.activation(rpart(k, 2 * i), zbank(k, i), Relu, scale=CS).then_inc(S["rr%d" % k], 1)
+            sc.activation(rpart(k, 2 * i + 1), zbank(k, i), Relu, scale=-CS).then_inc(S["rr%d" % k], 1)
+
+    def tcol(k, b):
+        return T.t_sb[:, (k - 1) * W + b:k * W:4]
+
+    def quant_t(k):
+        v.wait_ge(S["tl%d" % k], 4)
+        v.quantize_mx(T.tq[:, _cols(k)], T.tsc[:, _cols(k)],
+                      T.t_sb[:, (k - 1) * W:k * W]).then_inc(S["tqd%d" % k], 1)
+
+    v.memset(T.ones[:], 1.0).then_inc(S.s_ones, 1)
+    g.wait_ge(S.s_ones, 1)
+    g.affine_select(T.eye[:], T.ones[:], [[-1, EW]], AluOpType.is_equal, 0.0, 3, 4).then_inc(S.s_eye, 1)
+
+    quant_b(1)
+    v.wait_ge(S.ld_a, 16)
+    v.quantize_mx(T.aq[:], T.asc[:], T.a_sb[:]).then_inc(S.qa, 1)
+    products(1)
+    v.wait_ge(S.zm1_0, 1)
+    v.tensor_scalar(tcol(1, 0), zbank(1, 0), 0.0, CS, AluOpType.max, AluOpType.mult).then_inc(S.tl1, 1)
+    v.tensor_scalar(tcol(1, 1), zbank(1, 0), -CS, 0.0, AluOpType.mult, AluOpType.max).then_inc(S.tl1, 1)
+    sc.wait_ge(S.zm1_1, 1)
+    sc.activation(tcol(1, 2), zbank(1, 1), Relu, scale=CS).then_inc(S.tl1, 1)
+    sc.activation(tcol(1, 3), zbank(1, 1), Relu, scale=-CS).then_inc(S.tl1, 1)
+    quant_t(1)
+
+    quant_b(2)
+    products(2)
+    signs(2)
+    v.wait_ge(S.s_eye, 1)
+    for b in range(4):
+        v.quantize_mx(T.sq[:, b * NC:(b + 1) * NC], T.ssc[:, b * NC:(b + 1) * NC],
+                      T.eye[:, 3 - b:3 - b + W]).then_inc(S.qs, 1)
+    quant_b(3)
+    products(3)
+    signs(3)
+
+    for k in range(2, N + 1):
+        te.wait_ge(S["arc%d" % (k - 1)], n_in)
+        te.wait_ge(S["ars%d" % (k - 1)], n_in)
+        if k == 2:
+            te.wait_ge(S.qs, 4)
+        else:
+            te.wait_ge(S["tl%d" % (k - 1)], 4)
+        v.wait_ge(S["rr%d" % k], 4)
+        for b in range(4):
+            dbank = T.dp[:, b * BANK:b * BANK + NC]
+            te.matmul_mx(dbank, T.sq[:, b * NC:(b + 1) * NC], T.ssc[:, b * NC:(b + 1) * NC],
+                         T.lq[:, _cols(k - 1)], T.lsc[:, _cols(k - 1)],
+                         True, True).then_inc(S["dm%d_%d" % (k, b)], 1)
+            v.wait_ge(S["dm%d_%d" % (k, b)], 1)
+            out = tcol(k, b) if k < N else T.y_sb[:, b:W:4]
+            v.tensor_tensor(out, dbank, rpart(k, b), AluOpType.add).then_inc(S["tl%d" % k], 1)
+        if k < N:
+            quant_t(k)
+        if k + 2 <= N:
+            quant_b(k + 2)
+            products(k + 2)
+            signs(k + 2)
+
+    left = 0
+    for k in range(1, N):
+        g.wait_ge(S["tqd%d" % k], 1)
+        if RELAY_PLANE_FIRST and out_via is not None:
+            left += _put_plane(g, T, topo, core, nxt, k, T.tsc)
+            left += _put_codes(g, T, topo, core, nxt, k, T.tq)
+        else:
+            left += _put_codes(g, T, topo, core, nxt, k, T.tq)
+            left += _put_plane(g, T, topo, core, nxt, k, T.tsc)
+    g.wait_ge(S.sent, left)
+
+    sy.wait_ge(S["tl%d" % N], 4)
+    sy.dma_start(T.y[:], T.y_sb[:]).then_inc(S.stored, 16)
+    sy.wait_ge(S.stored, 16)

@@ -6,10 +6,7 @@ NC = 128
 BANK = 512
 CS = 0.031
 EW = 520
-
-ON_ENGINES = 16
-OFF_ENGINES = 8
-RELAY_PLANE_FIRST = False
+PB = 3
 
 SCRATCH = {
     "a_sb": ("sbuf", [128, 2 * W], "bfloat16"),
@@ -18,15 +15,15 @@ SCRATCH = {
     "asc": ("sbuf", [128, 2 * NC], "uint8"),
     "bq": ("sbuf", [128, N * NC], "float8_e4m3fn_x4"),
     "bsc": ("sbuf", [128, N * NC], "uint8"),
-    "ones": ("sbuf", [128, EW], "bfloat16"),
+    "ident": ("sbuf", [128, NC], "bfloat16"),
     "eye": ("sbuf", [128, EW], "bfloat16"),
-    "sq": ("sbuf", [128, 4 * NC], "float8_e4m3fn_x4"),
-    "ssc": ("sbuf", [128, 4 * NC], "uint8"),
+    "sq": ("sbuf", [128, 3 * NC], "float8_e4m3fn_x4"),
+    "ssc": ("sbuf", [128, 3 * NC], "uint8"),
     "t_sb": ("sbuf", [128, (N - 1) * W], "bfloat16"),
-    "tq": ("sbuf", [128, (N - 1) * NC], "float8_e4m3fn_x4"),
-    "tsc": ("sbuf", [128, (N - 1) * NC], "uint8"),
-    "lq": ("sbuf", [128, (N - 1) * NC], "float8_e4m3fn_x4"),
-    "lsc": ("sbuf", [128, (N - 1) * NC], "uint8"),
+    "tq": ("sbuf", [128, N * NC], "float8_e4m3fn_x4"),
+    "tsc": ("sbuf", [128, N * NC], "uint8"),
+    "lq": ("sbuf", [128, N * NC], "float8_e4m3fn_x4"),
+    "lsc": ("sbuf", [128, N * NC], "uint8"),
     "r_sb": ("sbuf", [128, (N - 1) * 4 * NC], "float32"),
     "y_sb": ("sbuf", [128, W], "float32"),
     "zp": ("psum", [128, 4 * BANK], "float32"),
@@ -34,86 +31,87 @@ SCRATCH = {
 }
 
 SEMAPHORES = (
-    ["ld_a", "ld_b1", "ld_b2", "ld_b3", "s_ones", "s_eye", "qa", "qs", "sent", "stored"]
+    ["ld_a0", "ld_a1", "ld_b1", "ld_b2", "ld_b3", "s_zero", "s_id", "s_eye", "qa0", "qa1", "qs", "sent", "stored"]
     + ["qb%d" % k for k in range(1, N + 1)]
     + ["zm%d_%d" % (k, i) for k in range(1, N + 1) for i in range(2)]
     + ["tl%d" % k for k in range(1, N + 1)]
     + ["rr%d" % k for k in range(2, N + 1)]
     + ["dm%d_%d" % (k, b) for k in range(2, N + 1) for b in range(4)]
-    + ["tqd%d" % k for k in range(1, N)]
-    + ["arc%d" % k for k in range(1, N)]
-    + ["ars%d" % k for k in range(1, N)]
+    + ["tqd%d" % k for k in range(0, N)]
+    + ["arc%d" % k for k in range(0, N)]
+    + ["ars%d" % k for k in range(0, N)]
 )
 
 
 def _engines(topo, src, dst):
-    allowed = topo.mask(src, dst)
-    bits = [e for e in range(allowed.bit_length()) if (allowed >> e) & 1]
-    want = ON_ENGINES if topo.chip(src) == topo.chip(dst) else OFF_ENGINES
-    n = min(want, len(bits))
-    step = len(bits) // n
-    m = 0
-    for e in bits[::step][:n]:
-        m |= 1 << e
-    return m, n
+    m = topo.mask(src, dst)
+    return m, sum((m >> e) & 1 for e in range(m.bit_length()))
 
 
 def _routes(cores, topo):
     out = []
     for r in range(N):
         src, dst = cores[r], cores[(r + 1) % N]
-        via = None
+        vc = vp = None
         if not topo.may_write(src, dst):
             cand = [c for c in range(topo.CORES_PER_CHIP * topo.CHIPS)
                     if topo.chip(c) == topo.chip(src) and c not in cores and topo.may_write(c, dst)]
             cand.sort(key=lambda c: (topo.die(c) != topo.die(src), c))
-            via = cand[0]
-        out.append((src, via, dst))
+            vc, vp = cand[0], cand[1]
+        out.append((src, vc, vp, dst))
     return out
 
 
 def _cols(k):
-    return slice((k - 1) * NC, k * NC)
+    return slice(k * NC, (k + 1) * NC)
 
 
-def _put_codes(g, T, topo, me, dst, k, src_buf):
+def _partner(cores, topo, c):
+    return [x for x in cores if x != c and topo.chip(x) == topo.chip(c)][0]
+
+
+def _both(topo, me, dst, later):
+    m = topo.mask(me, dst) & topo.mask(me, later)
+    return m, sum((m >> e) & 1 for e in range(m.bit_length()))
+
+
+def _put_codes(g, T, topo, me, dst, k, src_buf, eng=None):
     rid, pid, _se = topo.addr(dst)
-    m, n = _engines(topo, me, dst)
+    m, n = eng if eng is not None else _engines(topo, me, dst)
     g.remote_dma(T.lq[:, _cols(k)].bitcast(dt.uint8), src_buf[:, _cols(k)].bitcast(dt.uint8),
                  T.sem["arc%d" % k], T.sem.sent, pid, rid, m)
     return n
 
 
-def _put_plane(g, T, topo, me, dst, k, src_buf):
+def _put_plane(g, T, topo, me, dst, k, src_buf, eng=None):
     rid, pid, _se = topo.addr(dst)
-    m, n = _engines(topo, me, dst)
+    m, n = eng if eng is not None else _engines(topo, me, dst)
     g.remote_dma(T.lsc[:, _cols(k)], src_buf[:, _cols(k)], T.sem["ars%d" % k], T.sem.sent, pid, rid, m)
     return n
 
 
-def _forward(g, core, T, topo, src, dst):
+def _forward(g, core, T, topo, src, dst, codes):
     n_in = _engines(topo, src, core)[1]
+    mate = _partner(list(T.cores), topo, src)
     left = 0
-    for k in range(1, N):
-        if RELAY_PLANE_FIRST:
-            g.wait_ge(T.sem["ars%d" % k], n_in)
-            left += _put_plane(g, T, topo, core, dst, k, T.lsc)
+    for k in range(0, N):
+        to = mate if k == 0 else dst
+        eng = _both(topo, core, mate, dst) if k == 0 else None
+        if codes:
             g.wait_ge(T.sem["arc%d" % k], n_in)
-            left += _put_codes(g, T, topo, core, dst, k, T.lq)
+            left += _put_codes(g, T, topo, core, to, k, T.lq, eng)
         else:
-            g.wait_ge(T.sem["arc%d" % k], n_in)
-            left += _put_codes(g, T, topo, core, dst, k, T.lq)
             g.wait_ge(T.sem["ars%d" % k], n_in)
-            left += _put_plane(g, T, topo, core, dst, k, T.lsc)
+            left += _put_plane(g, T, topo, core, to, k, T.lsc, eng)
     g.wait_ge(T.sem.sent, left)
 
 
 def rank_program(g, core, T, topo):
     cores = list(T.cores)
     routes = _routes(cores, topo)
-    for src, via, dst in routes:
-        if via == core:
-            _forward(g, core, T, topo, src, dst)
+    for src, vc, vp, dst in routes:
+        if vc == core or vp == core:
+            _forward(g, core, T, topo, src, dst, vc == core)
             return
     rank = T.rank_of(core)
     if rank is None:
@@ -123,10 +121,16 @@ def rank_program(g, core, T, topo):
     v, te, sc, sy = g.vector, g.tensor, g.scalar, g.sync
     Relu = ActivationFunctionType.Relu
 
-    _src, out_via, out_dst = routes[rank]
-    nxt = out_dst if out_via is None else out_via
-    in_src, in_via, _dst = routes[(rank - 1) % N]
-    n_in = _engines(topo, in_src if in_via is None else in_via, core)[1]
+    _src, out_vc, out_vp, out_dst = routes[rank]
+    nxt_c = out_dst if out_vc is None else out_vc
+    nxt_p = out_dst if out_vp is None else out_vp
+    in_src, in_vc, in_vp, _dst = routes[(rank - 1) % N]
+    n_in_c = _engines(topo, in_src if in_vc is None else in_vc, core)[1]
+    n_in_p = _engines(topo, in_src if in_vp is None else in_vp, core)[1]
+    mate = _partner(cores, topo, core)
+    _ms, m_vc, m_vp, m_dst = routes[T.rank_of(mate)]
+    n0_c = _engines(topo, mate, core)[1] if m_vc is None else _both(topo, m_vc, core, m_dst)[1]
+    n0_p = _engines(topo, mate, core)[1] if m_vp is None else _both(topo, m_vp, core, m_dst)[1]
 
     def pos(k):
         return (N - k) % N
@@ -141,10 +145,10 @@ def rank_program(g, core, T, topo):
             p += run
         return n
 
-    sy.dma_start(T.a_sb[:], T.a[:]).then_inc(S.ld_a, 16)
-    groups = [(N - 1, N, S.ld_b1, sc), (N - 3, N - 1, S.ld_b2, sy), (0, N - 3, S.ld_b3, sy)]
-    loaded = []
-    for p0, p1, sem, q in groups:
+    sy.dma_start(T.a_sb[:, 0:W], T.a[:, 0:W]).then_inc(S.ld_a0, 16)
+    loaded = [(N - 1, N, S.ld_b1, load(sc, N - 1, N, S.ld_b1))]
+    sy.dma_start(T.a_sb[:, W:2 * W], T.a[:, W:2 * W]).then_inc(S.ld_a1, 16)
+    for p0, p1, sem, q in [(N - 3, N - 1, S.ld_b2, sy), (0, N - 3, S.ld_b3, sy)]:
         loaded.append((p0, p1, sem, load(q, p0, p1, sem)))
 
     def quant_b(k):
@@ -162,13 +166,13 @@ def rank_program(g, core, T, topo):
     def products(k):
         p = pos(k)
         te.wait_ge(S["qb%d" % k], 1)
-        if k == 1:
-            te.wait_ge(S.qa, 1)
-        elif k == 3:
+        if k == 3:
             te.wait_ge(S.tl1, 4)
         elif k > 3:
             te.wait_ge(S["rr%d" % (k - 2)], 4)
         for i in range(2):
+            if k == 1:
+                te.wait_ge(S["qa%d" % i], 1)
             te.matmul_mx(zbank(k, i), T.aq[:, i * NC:(i + 1) * NC], T.asc[:, i * NC:(i + 1) * NC],
                          T.bq[:, p * NC:(p + 1) * NC], T.bsc[:, p * NC:(p + 1) * NC],
                          True, True).then_inc(S["zm%d_%d" % (k, i)], 1)
@@ -191,45 +195,60 @@ def rank_program(g, core, T, topo):
         v.quantize_mx(T.tq[:, _cols(k)], T.tsc[:, _cols(k)],
                       T.t_sb[:, (k - 1) * W:k * W]).then_inc(S["tqd%d" % k], 1)
 
-    v.memset(T.ones[:], 1.0).then_inc(S.s_ones, 1)
-    g.wait_ge(S.s_ones, 1)
-    g.affine_select(T.eye[:], T.ones[:], [[-1, EW]], AluOpType.is_equal, 0.0, 3, 4).then_inc(S.s_eye, 1)
+    g.iota(T.ident[:], [[-1, NC]], 0, 1, allow_small_or_imprecise_dtypes=True).then_inc(S.s_id, 1)
+    v.memset(T.eye[:], 0.0).then_inc(S.s_zero, 1)
+    v.wait_ge(S.s_zero, 1)
+    v.wait_ge(S.s_id, 1)
+    v.tensor_scalar(T.eye[:, 3:W:4], T.ident[:], 0.0, None, AluOpType.is_equal).then_inc(S.s_eye, 1)
+    v.wait_ge(S.s_eye, 1)
+    v.quantize_mx(T.tq[:, _cols(0)], T.tsc[:, _cols(0)], T.eye[:, 3 - PB:3 - PB + W]).then_inc(S.tqd0, 1)
 
     quant_b(1)
-    v.wait_ge(S.ld_a, 16)
-    v.quantize_mx(T.aq[:], T.asc[:], T.a_sb[:]).then_inc(S.qa, 1)
+    for i in range(2):
+        v.wait_ge(S["ld_a%d" % i], 16)
+        v.quantize_mx(T.aq[:, i * NC:(i + 1) * NC], T.asc[:, i * NC:(i + 1) * NC],
+                      T.a_sb[:, i * W:(i + 1) * W]).then_inc(S["qa%d" % i], 1)
     products(1)
-    v.wait_ge(S.zm1_0, 1)
-    v.tensor_scalar(tcol(1, 0), zbank(1, 0), 0.0, CS, AluOpType.max, AluOpType.mult).then_inc(S.tl1, 1)
-    v.tensor_scalar(tcol(1, 1), zbank(1, 0), -CS, 0.0, AluOpType.mult, AluOpType.max).then_inc(S.tl1, 1)
-    sc.wait_ge(S.zm1_1, 1)
-    sc.activation(tcol(1, 2), zbank(1, 1), Relu, scale=CS).then_inc(S.tl1, 1)
-    sc.activation(tcol(1, 3), zbank(1, 1), Relu, scale=-CS).then_inc(S.tl1, 1)
+    sc.wait_ge(S.zm1_0, 1)
+    sc.activation(tcol(1, 0), zbank(1, 0), Relu, scale=CS).then_inc(S.tl1, 1)
+    sc.activation(tcol(1, 1), zbank(1, 0), Relu, scale=-CS).then_inc(S.tl1, 1)
+    v.wait_ge(S.zm1_1, 1)
+    v.tensor_scalar(tcol(1, 2), zbank(1, 1), 0.0, CS, AluOpType.max, AluOpType.mult).then_inc(S.tl1, 1)
+    v.tensor_scalar(tcol(1, 3), zbank(1, 1), -CS, 0.0, AluOpType.mult, AluOpType.max).then_inc(S.tl1, 1)
     quant_t(1)
 
     quant_b(2)
     products(2)
     signs(2)
-    v.wait_ge(S.s_eye, 1)
-    for b in range(4):
-        v.quantize_mx(T.sq[:, b * NC:(b + 1) * NC], T.ssc[:, b * NC:(b + 1) * NC],
+    own = [b for b in range(4) if b != PB]
+    for j, b in enumerate(own):
+        v.quantize_mx(T.sq[:, j * NC:(j + 1) * NC], T.ssc[:, j * NC:(j + 1) * NC],
                       T.eye[:, 3 - b:3 - b + W]).then_inc(S.qs, 1)
     quant_b(3)
     products(3)
     signs(3)
 
+    def pick(b):
+        if b == PB:
+            return T.lq[:, _cols(0)], T.lsc[:, _cols(0)]
+        j = own.index(b)
+        return T.sq[:, j * NC:(j + 1) * NC], T.ssc[:, j * NC:(j + 1) * NC]
+
     for k in range(2, N + 1):
-        te.wait_ge(S["arc%d" % (k - 1)], n_in)
-        te.wait_ge(S["ars%d" % (k - 1)], n_in)
+        te.wait_ge(S["arc%d" % (k - 1)], n_in_c)
+        te.wait_ge(S["ars%d" % (k - 1)], n_in_p)
         if k == 2:
-            te.wait_ge(S.qs, 4)
+            te.wait_ge(S.qs, len(own))
         else:
             te.wait_ge(S["tl%d" % (k - 1)], 4)
         v.wait_ge(S["rr%d" % k], 4)
-        for b in range(4):
+        for b in own + [PB]:
+            if k == 2 and b == PB:
+                te.wait_ge(S.arc0, n0_c)
+                te.wait_ge(S.ars0, n0_p)
             dbank = T.dp[:, b * BANK:b * BANK + NC]
-            te.matmul_mx(dbank, T.sq[:, b * NC:(b + 1) * NC], T.ssc[:, b * NC:(b + 1) * NC],
-                         T.lq[:, _cols(k - 1)], T.lsc[:, _cols(k - 1)],
+            pc, pp = pick(b)
+            te.matmul_mx(dbank, pc, pp, T.lq[:, _cols(k - 1)], T.lsc[:, _cols(k - 1)],
                          True, True).then_inc(S["dm%d_%d" % (k, b)], 1)
             v.wait_ge(S["dm%d_%d" % (k, b)], 1)
             out = tcol(k, b) if k < N else T.y_sb[:, b:W:4]
@@ -242,14 +261,10 @@ def rank_program(g, core, T, topo):
             signs(k + 2)
 
     left = 0
-    for k in range(1, N):
+    for k in range(0, N):
         g.wait_ge(S["tqd%d" % k], 1)
-        if RELAY_PLANE_FIRST and out_via is not None:
-            left += _put_plane(g, T, topo, core, nxt, k, T.tsc)
-            left += _put_codes(g, T, topo, core, nxt, k, T.tq)
-        else:
-            left += _put_codes(g, T, topo, core, nxt, k, T.tq)
-            left += _put_plane(g, T, topo, core, nxt, k, T.tsc)
+        left += _put_codes(g, T, topo, core, mate if k == 0 and out_vc is None else nxt_c, k, T.tq)
+        left += _put_plane(g, T, topo, core, mate if k == 0 and out_vp is None else nxt_p, k, T.tsc)
     g.wait_ge(S.sent, left)
 
     sy.wait_ge(S["tl%d" % N], 4)

from concourse.mybir import dt, AluOpType, ActivationFunctionType

N = 6
W = 512
NC = 128
BANK = 512
CS = 0.031
EW = 520
PB = 3

SCRATCH = {
    "a_sb": ("sbuf", [128, 2 * W], "bfloat16"),
    "b_sb": ("sbuf", [128, N * W], "bfloat16"),
    "aq": ("sbuf", [128, 2 * NC], "float8_e4m3fn_x4"),
    "asc": ("sbuf", [128, 2 * NC], "uint8"),
    "bq": ("sbuf", [128, N * NC], "float8_e4m3fn_x4"),
    "bsc": ("sbuf", [128, N * NC], "uint8"),
    "ident": ("sbuf", [128, NC], "bfloat16"),
    "eye": ("sbuf", [128, EW], "bfloat16"),
    "sq": ("sbuf", [128, 3 * NC], "float8_e4m3fn_x4"),
    "ssc": ("sbuf", [128, 3 * NC], "uint8"),
    "t_sb": ("sbuf", [128, (N - 1) * W], "bfloat16"),
    "tq": ("sbuf", [128, N * NC], "float8_e4m3fn_x4"),
    "tsc": ("sbuf", [128, N * NC], "uint8"),
    "lq": ("sbuf", [128, N * NC], "float8_e4m3fn_x4"),
    "lsc": ("sbuf", [128, N * NC], "uint8"),
    "r_sb": ("sbuf", [128, (N - 1) * 4 * NC], "float32"),
    "y_sb": ("sbuf", [128, W], "float32"),
    "zp": ("psum", [128, 4 * BANK], "float32"),
    "dp": ("psum", [128, 4 * BANK], "float32"),
}

SEMAPHORES = (
    ["ld_a0", "ld_a1", "ld_b1", "ld_b2", "ld_b3", "s_zero", "s_id", "s_eye", "qa0", "qa1", "qs", "sent", "stored"]
    + ["qb%d" % k for k in range(1, N + 1)]
    + ["zm%d_%d" % (k, i) for k in range(1, N + 1) for i in range(2)]
    + ["tl%d" % k for k in range(1, N + 1)]
    + ["rr%d" % k for k in range(2, N + 1)]
    + ["dm%d_%d" % (k, b) for k in range(2, N + 1) for b in range(4)]
    + ["tqd%d" % k for k in range(0, N)]
    + ["arc%d" % k for k in range(0, N)]
    + ["ars%d" % k for k in range(0, N)]
)


def _engines(topo, src, dst):
    m = topo.mask(src, dst)
    return m, sum((m >> e) & 1 for e in range(m.bit_length()))


def _routes(cores, topo):
    out = []
    for r in range(N):
        src, dst = cores[r], cores[(r + 1) % N]
        vc = vp = None
        if not topo.may_write(src, dst):
            cand = [c for c in range(topo.CORES_PER_CHIP * topo.CHIPS)
                    if topo.chip(c) == topo.chip(src) and c not in cores and topo.may_write(c, dst)]
            cand.sort(key=lambda c: (topo.die(c) != topo.die(src), c))
            vc, vp = cand[0], cand[1]
        out.append((src, vc, vp, dst))
    return out


def _cols(k):
    return slice(k * NC, (k + 1) * NC)


def _partner(cores, topo, c):
    return [x for x in cores if x != c and topo.chip(x) == topo.chip(c)][0]


def _both(topo, me, dst, later):
    m = topo.mask(me, dst) & topo.mask(me, later)
    return m, sum((m >> e) & 1 for e in range(m.bit_length()))


def _put_codes(g, T, topo, me, dst, k, src_buf, eng=None):
    rid, pid, _se = topo.addr(dst)
    m, n = eng if eng is not None else _engines(topo, me, dst)
    g.remote_dma(T.lq[:, _cols(k)].bitcast(dt.uint8), src_buf[:, _cols(k)].bitcast(dt.uint8),
                 T.sem["arc%d" % k], T.sem.sent, pid, rid, m)
    return n


def _put_plane(g, T, topo, me, dst, k, src_buf, eng=None):
    rid, pid, _se = topo.addr(dst)
    m, n = eng if eng is not None else _engines(topo, me, dst)
    g.remote_dma(T.lsc[:, _cols(k)], src_buf[:, _cols(k)], T.sem["ars%d" % k], T.sem.sent, pid, rid, m)
    return n


def _forward(g, core, T, topo, src, dst, codes):
    n_in = _engines(topo, src, core)[1]
    mate = _partner(list(T.cores), topo, src)
    left = 0
    for k in range(0, N):
        to = mate if k == 0 else dst
        eng = _both(topo, core, mate, dst) if k == 0 else None
        if codes:
            g.wait_ge(T.sem["arc%d" % k], n_in)
            left += _put_codes(g, T, topo, core, to, k, T.lq, eng)
        else:
            g.wait_ge(T.sem["ars%d" % k], n_in)
            left += _put_plane(g, T, topo, core, to, k, T.lsc, eng)
    g.wait_ge(T.sem.sent, left)


def rank_program(g, core, T, topo):
    cores = list(T.cores)
    routes = _routes(cores, topo)
    for src, vc, vp, dst in routes:
        if vc == core or vp == core:
            _forward(g, core, T, topo, src, dst, vc == core)
            return
    rank = T.rank_of(core)
    if rank is None:
        return

    S = T.sem
    v, te, sc, sy = g.vector, g.tensor, g.scalar, g.sync
    Relu = ActivationFunctionType.Relu

    _src, out_vc, out_vp, out_dst = routes[rank]
    nxt_c = out_dst if out_vc is None else out_vc
    nxt_p = out_dst if out_vp is None else out_vp
    in_src, in_vc, in_vp, _dst = routes[(rank - 1) % N]
    n_in_c = _engines(topo, in_src if in_vc is None else in_vc, core)[1]
    n_in_p = _engines(topo, in_src if in_vp is None else in_vp, core)[1]
    mate = _partner(cores, topo, core)
    _ms, m_vc, m_vp, m_dst = routes[T.rank_of(mate)]
    n0_c = _engines(topo, mate, core)[1] if m_vc is None else _both(topo, m_vc, core, m_dst)[1]
    n0_p = _engines(topo, mate, core)[1] if m_vp is None else _both(topo, m_vp, core, m_dst)[1]

    def pos(k):
        return (N - k) % N

    def load(q, p0, p1, sem):
        n, p = 0, p0
        while p < p1:
            c = (rank + p) % N
            run = min(p1 - p, N - c)
            q.dma_start(T.b_sb[:, p * W:(p + run) * W], T.b[:, c * W:(c + run) * W]).then_inc(sem, 16)
            n += 16
            p += run
        return n

    sy.dma_start(T.a_sb[:, 0:W], T.a[:, 0:W]).then_inc(S.ld_a0, 16)
    loaded = [(N - 1, N, S.ld_b1, load(sc, N - 1, N, S.ld_b1))]
    sy.dma_start(T.a_sb[:, W:2 * W], T.a[:, W:2 * W]).then_inc(S.ld_a1, 16)
    for p0, p1, sem, q in [(N - 3, N - 1, S.ld_b2, sy), (0, N - 3, S.ld_b3, sy)]:
        loaded.append((p0, p1, sem, load(q, p0, p1, sem)))

    def quant_b(k):
        p = pos(k)
        for p0, p1, sem, n in loaded:
            if p0 <= p < p1:
                v.wait_ge(sem, n)
        v.quantize_mx(T.bq[:, p * NC:(p + 1) * NC], T.bsc[:, p * NC:(p + 1) * NC],
                      T.b_sb[:, p * W:(p + 1) * W]).then_inc(S["qb%d" % k], 1)

    def zbank(k, i):
        j = 2 * ((k - 1) % 2) + i
        return T.zp[:, j * BANK:j * BANK + NC]

    def products(k):
        p = pos(k)
        te.wait_ge(S["qb%d" % k], 1)
        if k == 3:
            te.wait_ge(S.tl1, 4)
        elif k > 3:
            te.wait_ge(S["rr%d" % (k - 2)], 4)
        for i in range(2):
            if k == 1:
                te.wait_ge(S["qa%d" % i], 1)
            te.matmul_mx(zbank(k, i), T.aq[:, i * NC:(i + 1) * NC], T.asc[:, i * NC:(i + 1) * NC],
                         T.bq[:, p * NC:(p + 1) * NC], T.bsc[:, p * NC:(p + 1) * NC],
                         True, True).then_inc(S["zm%d_%d" % (k, i)], 1)

    def rpart(k, b):
        j = (k - 2) * 4 + b
        return T.r_sb[:, j * NC:(j + 1) * NC]

    def signs(k):
        for i in range(2):
            sc.wait_ge(S["zm%d_%d" % (k, i)], 1)
            sc.activation(rpart(k, 2 * i), zbank(k, i), Relu, scale=CS).then_inc(S["rr%d" % k], 1)
            sc.activation(rpart(k, 2 * i + 1), zbank(k, i), Relu, scale=-CS).then_inc(S["rr%d" % k], 1)

    def tcol(k, b):
        return T.t_sb[:, (k - 1) * W + b:k * W:4]

    def quant_t(k):
        v.wait_ge(S["tl%d" % k], 4)
        v.quantize_mx(T.tq[:, _cols(k)], T.tsc[:, _cols(k)],
                      T.t_sb[:, (k - 1) * W:k * W]).then_inc(S["tqd%d" % k], 1)

    g.iota(T.ident[:], [[-1, NC]], 0, 1, allow_small_or_imprecise_dtypes=True).then_inc(S.s_id, 1)
    v.memset(T.eye[:], 0.0).then_inc(S.s_zero, 1)
    v.wait_ge(S.s_zero, 1)
    v.wait_ge(S.s_id, 1)
    v.tensor_scalar(T.eye[:, 3:W:4], T.ident[:], 0.0, None, AluOpType.is_equal).then_inc(S.s_eye, 1)
    v.wait_ge(S.s_eye, 1)
    v.quantize_mx(T.tq[:, _cols(0)], T.tsc[:, _cols(0)], T.eye[:, 3 - PB:3 - PB + W]).then_inc(S.tqd0, 1)

    quant_b(1)
    for i in range(2):
        v.wait_ge(S["ld_a%d" % i], 16)
        v.quantize_mx(T.aq[:, i * NC:(i + 1) * NC], T.asc[:, i * NC:(i + 1) * NC],
                      T.a_sb[:, i * W:(i + 1) * W]).then_inc(S["qa%d" % i], 1)
    products(1)
    sc.wait_ge(S.zm1_0, 1)
    sc.activation(tcol(1, 0), zbank(1, 0), Relu, scale=CS).then_inc(S.tl1, 1)
    sc.activation(tcol(1, 1), zbank(1, 0), Relu, scale=-CS).then_inc(S.tl1, 1)
    v.wait_ge(S.zm1_1, 1)
    v.tensor_scalar(tcol(1, 2), zbank(1, 1), 0.0, CS, AluOpType.max, AluOpType.mult).then_inc(S.tl1, 1)
    v.tensor_scalar(tcol(1, 3), zbank(1, 1), -CS, 0.0, AluOpType.mult, AluOpType.max).then_inc(S.tl1, 1)
    quant_t(1)

    quant_b(2)
    products(2)
    signs(2)
    own = [b for b in range(4) if b != PB]
    for j, b in enumerate(own):
        v.quantize_mx(T.sq[:, j * NC:(j + 1) * NC], T.ssc[:, j * NC:(j + 1) * NC],
                      T.eye[:, 3 - b:3 - b + W]).then_inc(S.qs, 1)
    quant_b(3)
    products(3)
    signs(3)

    def pick(b):
        if b == PB:
            return T.lq[:, _cols(0)], T.lsc[:, _cols(0)]
        j = own.index(b)
        return T.sq[:, j * NC:(j + 1) * NC], T.ssc[:, j * NC:(j + 1) * NC]

    for k in range(2, N + 1):
        te.wait_ge(S["arc%d" % (k - 1)], n_in_c)
        te.wait_ge(S["ars%d" % (k - 1)], n_in_p)
        if k == 2:
            te.wait_ge(S.qs, len(own))
        else:
            te.wait_ge(S["tl%d" % (k - 1)], 4)
        v.wait_ge(S["rr%d" % k], 4)
        for b in own + [PB]:
            if k == 2 and b == PB:
                te.wait_ge(S.arc0, n0_c)
                te.wait_ge(S.ars0, n0_p)
            dbank = T.dp[:, b * BANK:b * BANK + NC]
            pc, pp = pick(b)
            te.matmul_mx(dbank, pc, pp, T.lq[:, _cols(k - 1)], T.lsc[:, _cols(k - 1)],
                         True, True).then_inc(S["dm%d_%d" % (k, b)], 1)
            v.wait_ge(S["dm%d_%d" % (k, b)], 1)
            out = tcol(k, b) if k < N else T.y_sb[:, b:W:4]
            v.tensor_tensor(out, dbank, rpart(k, b), AluOpType.add).then_inc(S["tl%d" % k], 1)
        if k < N:
            quant_t(k)
        if k + 2 <= N:
            quant_b(k + 2)
            products(k + 2)
            signs(k + 2)

    left = 0
    for k in range(0, N):
        g.wait_ge(S["tqd%d" % k], 1)
        left += _put_codes(g, T, topo, core, mate if k == 0 and out_vc is None else nxt_c, k, T.tq)
        left += _put_plane(g, T, topo, core, mate if k == 0 and out_vp is None else nxt_p, k, T.tsc)
    g.wait_ge(S.sent, left)

    sy.wait_ge(S["tl%d" % N], 4)
    sy.dma_start(T.y[:], T.y_sb[:]).then_inc(S.stored, 16)
    sy.wait_ge(S.stored, 16)
